import numpy as np
import ml_dtypes


def mxq(x, axis, fmt="e4m3"):
    dtype, down = {"e4m3": (ml_dtypes.float8_e4m3fn, 7), "e5m2": (ml_dtypes.float8_e5m2, 14)}[fmt]
    v = np.moveaxis(np.asarray(x, np.float32).astype(ml_dtypes.bfloat16).astype(np.float64), axis, -1)
    blocks = v.reshape(v.shape[:-1] + (-1, 32))
    amax = np.abs(blocks).max(-1, keepdims=True)
    byte = np.maximum(np.where(amax > 0, np.frexp(amax)[1] - 1 + 127, 0) - down, 1)
    scale = np.exp2(byte - 127.0)
    codes = (blocks / scale).astype(np.float32).astype(dtype).astype(np.float64)
    return np.moveaxis((codes * scale).reshape(v.shape), -1, axis)


WIDE = False


def mx_kscale(k):
    if not WIDE:
        return np.ones(k)
    levels = np.array([10, -10, 5, -5, 0])
    if k % 512:
        return np.exp2(np.random.permutation(np.resize(levels, k // 32))).repeat(32)
    a = np.empty((k // 512, 16))
    for p in range(k // 512):
        a[p, :8] = np.random.permutation(np.resize(levels, 8))
        for g in range(8):
            far = levels[np.abs(levels - a[p, g]) >= 10]
            a[p, g + 8] = far[np.random.randint(len(far))]
    return np.exp2(a.ravel()).repeat(32)


def f64(x):
    return np.asarray(x).astype(np.float64)


def striped(idx):
    return np.tile(idx.reshape(-1, 16).T, (8, 1)).astype(np.uint16)


def unstriped(offs):
    return offs[:16].T.reshape(-1).astype(np.int64)


E2M1 = np.array([0.0, 0.5, 1.0, 1.5, 2.0, 3.0, 4.0, 6.0, -0.0, -0.5, -1.0, -1.5, -2.0, -3.0, -4.0, -6.0])


def pack_weight(w, fmt):
    k, n = w.shape
    w = f64(np.asarray(w, np.float32).astype(ml_dtypes.bfloat16)).reshape(k // 32, 32, n)
    amax = np.abs(w).max(1)
    if fmt == "e4m3":
        byte = np.frexp(amax)[1] - 1 + 127 - 7
    else:
        mant, ex = np.frexp(amax / 6.0)
        byte = np.where(mant > 0.5, ex, ex - 1) + 127
    byte = np.clip(np.where(amax > 0, byte, 1), 1, 254)
    scaled = (w * np.exp2(127.0 - byte)[:, None, :]).reshape(k, n).astype(np.float32)
    by_word = np.ascontiguousarray(scaled.reshape(k // 512, 128, 4, n).transpose(0, 1, 3, 2))
    if fmt == "e4m3":
        words = by_word.astype(ml_dtypes.float8_e4m3fn).view(np.uint8)
    else:
        c = by_word.astype(ml_dtypes.float4_e2m1fn).view(np.uint8) & 0xF
        words = (c[..., 0::2] | (c[..., 1::2] << 4)).reshape(k // 512, 128, 2 * n)
    return np.ascontiguousarray(words), np.ascontiguousarray(byte.astype(np.uint8).reshape(k // 512, 16, n))


def unpack_weight(words, scales, fmt):
    g, _, n = scales.shape
    words = np.ascontiguousarray(words).reshape(g, 128, n, -1)
    if fmt == "e4m3":
        vals = words.view(ml_dtypes.float8_e4m3fn).astype(np.float64)
    else:
        nib = np.empty((g, 128, n, 4), np.uint8)
        nib[..., 0::2] = words & 0xF
        nib[..., 1::2] = words >> 4
        vals = E2M1[nib]
    vals = vals * np.repeat(np.exp2(scales.astype(np.float64) - 127.0), 8, axis=1)[..., None]
    return vals.transpose(0, 1, 3, 2).reshape(g * 512, n)


def gelu(v):
    return 0.5 * v * (1.0 + np.tanh(np.sqrt(2.0 / np.pi) * (v + 0.044715 * v**3)))


K, T, S, H, N = 1024, 2048, 1024, 512, 256

def setup_inputs():
    n = np.random.standard_normal
    s = mx_kscale(K)[:, None]
    u = mx_kscale(H)[:, None]
    d = {}
    d["tab_words"], d["tab_scales"] = pack_weight(n((K, T)) * s, "e4m3")
    d["tab2_words"], d["tab2_scales"] = pack_weight(n((K, T)) * s, "e4m3")
    d["offs"] = striped(np.random.permutation(T)[:S])
    d["offs2"] = striped(np.random.permutation(T)[:S])
    d["wa"] = (n((K, H)) / np.sqrt(K) / s).astype(np.float32)
    d["wb_words"], d["wb_scales"] = pack_weight(n((K, H)) / np.sqrt(K) / s, "e2m1")
    d["gT"] = (u / (1.0 + np.exp(-2.0 * n((H, T))))).astype(np.float32)
    d["wm"] = (n((H, N)) / np.sqrt(H) / u).astype(np.float32)
    return d

def reference(tab_words, tab_scales, tab2_words, tab2_scales, offs, offs2, wa, wb_words, wb_scales, gT, wm):
    v = unpack_weight(tab_words, tab_scales, "e4m3")[:, unstriped(offs)]
    v2 = unpack_weight(tab2_words, tab2_scales, "e4m3")[:, unstriped(offs2)]
    wb = unpack_weight(wb_words, wb_scales, "e2m1")
    g = f64(gT)[:, unstriped(offs)]
    a = mxq(f64(wa), 0, "e4m3").T @ v
    b = wb.T @ v2
    h = np.sqrt(np.square(a) + np.square(b)) * g
    return mxq(f64(wm), 0, "e4m3").T @ mxq(h, 0, "e4m3")

@@ -1,0 +1,271 @@
+from contextlib import ExitStack
+
+import concourse.mybir as mybir
+from concourse.masks import make_identity
+
+K, T, S, H, N = 1024, 2048, 1024, 512, 256
+FLOPS = 2 * (2 * K * H * S + H * N * S)
+
+F32 = mybir.dt.float32
+BF16 = mybir.dt.bfloat16
+I32 = mybir.dt.int32
+U32 = mybir.dt.uint32
+U16 = mybir.dt.uint16
+U8 = mybir.dt.uint8
+FP8X4 = mybir.dt.float8_e4m3fn_x4
+FP4X4 = mybir.dt.float4_e2m1fn_x4
+ACT = mybir.ActivationFunctionType
+MULT = mybir.AluOpType.mult
+
+P = 128
+PACK = 4
+PASSES = K // (P * PACK)
+TILES = S // P
+SLICES = [(0, 256), (256, 256), (512, 512)]
+V_ROW = 8
+MASK_RUNS = [(0, 512, None), (512, 256, "mag0_3"), (768, 256, "h_grouped1")]
+EARLY_TILES = 5
+HALF = S // 2
+HALF_TILES = HALF // P
+WA_SPLIT = 128
+GROUPS = [(0, 256), (256, 256), (512, 256), (768, 128), (896, 128)]
+INTERLEAVE_ON_VECTOR = (3, 4)
+COPY_OUT_ON_VECTOR = ()
+
+
+def picked(window, offsets, j0, n):
+    return window.indirect(offsets[:, j0 // 16 : (j0 + n) // 16])
+
+
+def interleave(copy, grouped, planes):
+    copy(
+        out=grouped.rearrange("p (c i) t -> p c t i", i=4),
+        in_=planes.rearrange("p t (c i) -> p c t i", i=4),
+    )
+
+
+def tile_list_masked_magnitude_mel_kernel(
+    tc, tab_words, tab_scales, tab2_words, tab2_scales, offs, offs2, wa, wb_words, wb_scales, gT, wm, out
+):
+    nc = tc.nc
+    with ExitStack() as ctx:
+        keep = ctx.enter_context(tc.tile_pool(name="keep", bufs=1))
+        psum = ctx.enter_context(tc.psum_pool(name="psum", bufs=1))
+
+        def held(shape, dtype, name, tag=None):
+            return keep.tile(shape, dtype, name=name, tag=tag or name, align_bytes=64)
+
+        def bank(b, shape):
+            return psum.tile(shape, F32, name=f"bank{b}")
+
+        idx = keep.tile([P, S // 16], U16, name="idx")
+        idx2 = keep.tile([P, S // 16], U16, name="idx2")
+        v_tab = [held([P, T], I32, f"v_tab{a}") for a in range(PASSES)]
+        v2_tab = [held([P, T], I32, f"v2_tab{a}") for a in range(PASSES)]
+        g_tab = [held([P, T], F32, f"g_tab{t}") for t in range(PACK)]
+        wa_raw = [held([P, PACK, H], F32, f"wa_raw{a}") for a in range(PASSES)]
+        wm_raw = held([P, PACK, N], F32, "wm_raw")
+        wb_codes = held([P, PASSES, H // 2], I32, "wb_codes")
+        v_tab_scales = held([P, T // 4], I32, "v_tab_scales")
+        v2_tab_scales = held([P, T // 4], I32, "v2_tab_scales")
+        wb_planes = held([P, PASSES, H // 4], I32, "wb_planes")
+        v2_plane1 = held([P, S // 4], I32, "v2_plane1")
+        v_codes = [held([P, S], U32, f"v_codes{a}") for a in range(PASSES)]
+        v2_codes = [held([P, S], U32, f"v2_codes{a}") for a in range(PASSES)]
+        v_planes = held([P, S], U8, "v_planes")
+        v2_planes = held([P, S], U8, "v2_planes")
+
+        nc.gpsimd.memset(v2_tab_scales[:], 0)
+        nc.vector.memset(wb_planes[:], 0)
+        nc.vector.memset(v_tab_scales[:], 0)
+        nc.vector.memset(v2_plane1[96:P, :], 0)
+        ident = held([P, P], F32, "ident")
+        make_identity(nc, ident[:])
+        warm = held([P, 1], F32, "warm")
+        nc.scalar.activation(warm[:], ident[:, 0:1], ACT.Sqrt)
+
+        def table_words(words, a):
+            return words[a].rearrange("p n t -> p (n t)").bitcast(I32)
+
+        def load_scales(queue, tile, scales, row):
+            for q in range(4):
+                queue.dma_start(
+                    tile[32 * q + row : 32 * q + row + 8, :], scales.bitcast(I32)[:, 4 * q : 4 * q + 4, :]
+                )
+
+        def load_wa(a):
+            nc.sync.dma_start(wa_raw[a][:], wa[512 * a : 512 * (a + 1), :].rearrange("(p j) r -> p j r", j=PACK))
+
+        def gather_words(dst, table, offsets, j0, n):
+            nc.vector.tensor_copy(dst[:, j0 : j0 + n], picked(table[:].bitcast(U32), offsets, j0, n))
+
+        def gather_scales(dst, table, offsets, j0, n):
+            nc.vector.tensor_copy(dst[:, j0 : j0 + n], picked(table[:].bitcast(U8), offsets, j0, n))
+
+        def quantize(grouped, width, name):
+            codes = held([P, width], U32, name + "_codes")
+            plane = held([P, width], U8, name + "_plane")
+            nc.vector.quantize_mx(
+                out=codes[:].bitcast(FP8X4), scales=plane[:], in_=grouped[:].rearrange("p w t -> p (w t)")
+            )
+            return codes, plane
+
+        nc.sync.dma_start(idx2[:], offs2)
+        nc.sync.dma_start(idx[:], offs)
+        load_scales(nc.sync, v2_tab_scales, tab2_scales, 0)
+        nc.sync.dma_start(v2_tab[0][:], table_words(tab2_words, 0))
+        nc.sync.dma_start(wb_codes[:], wb_words.bitcast(I32).rearrange("a p c -> p a c"))
+        for q in range(4):
+            nc.sync.dma_start(
+                wb_planes[32 * q : 32 * q + 4, :, :],
+                wb_scales.bitcast(I32)[:, 4 * q : 4 * q + 4, :].rearrange("a r c -> r a c"),
+            )
+        nc.sync.dma_start(v2_tab[1][:], table_words(tab2_words, 1))
+        gather_scales(v2_planes, v2_tab_scales, idx2, 0, S)
+        nc.sync.dma_start(v2_plane1[0:112, :], v2_planes[4:116, :].bitcast(I32))
+        load_wa(0)
+        load_scales(nc.sync, v_tab_scales, tab_scales, V_ROW)
+        load_wa(1)
+        for a in range(PASSES):
+            nc.sync.dma_start(v_tab[a][:], table_words(tab_words, a))
+        g_planes = gT.rearrange("(p t) c -> t p c", t=PACK)
+        nc.sync.dma_start(g_tab[0][:], g_planes[0])
+        nc.sync.dma_start(wm_raw[:], wm.rearrange("(p j) n -> p j n", j=PACK))
+        for t in range(1, PACK):
+            nc.sync.dma_start(g_tab[t][:], g_planes[t])
+
+        def real_pass(acc, i, a):
+            cols = slice(P * i, P * (i + 1))
+            nc.tensor.matmul_mx(
+                out=acc[:],
+                lhsT=v_codes[a][:, cols].bitcast(FP8X4),
+                lhsT_scale=v_planes[V_ROW + 4 * a : P, cols],
+                rhs=wa_mx[a][0][:].bitcast(FP8X4),
+                rhs_scale=wa_mx[a][1][:],
+                start=(a == 0),
+                stop=(a == PASSES - 1),
+            )
+
+        def imag_pass(acc, i, a):
+            cols = slice(P * i, P * (i + 1))
+            plane = v2_planes[:] if a == 0 else v2_plane1[:].bitcast(U8)
+            nc.tensor.matmul_mx(
+                out=acc[:],
+                lhsT=v2_codes[a][:, cols].bitcast(FP8X4),
+                lhsT_scale=plane[:, cols],
+                rhs=wb_codes[:, a, :].bitcast(FP4X4),
+                rhs_scale=wb_planes[:, a, :].bitcast(U8),
+                start=(a == 0),
+                stop=(a == PASSES - 1),
+            )
+
+        def square(dst, acc):
+            nc.scalar.activation(dst[:], acc[:].rearrange("p (m t) -> p t m", t=PACK), ACT.Square)
+
+        def turn(total, sq, i, t, first, last):
+            j = P * (i % HALF_TILES)
+            nc.tensor.matmul(
+                total[:, j : j + P], lhsT=sq[i][:, t, :], rhs=ident[:], is_transpose=True, start=first, stop=last
+            )
+
+        imag = [bank((i + 4) % 8, [P, H]) for i in range(TILES)]
+        for j0 in range(0, S, HALF):
+            gather_words(v2_codes[0], v2_tab[0], idx2, j0, HALF)
+            for i in range(j0 // P, (j0 + HALF) // P):
+                imag_pass(imag[i], i, 0)
+        imag_sq = [held([P, PACK, P], F32, f"imag_sq{i}") for i in range(TILES)]
+        for j0, n in SLICES:
+            gather_words(v2_codes[1], v2_tab[1], idx2, j0, n)
+            for i in range(j0 // P, (j0 + n) // P):
+                imag_pass(imag[i], i, 1)
+                square(imag_sq[i], imag[i])
+
+        totals = [bank(4 + t, [P, HALF]) for t in range(PACK)]
+        for i in range(HALF_TILES):
+            for t in range(PACK):
+                turn(totals[t], imag_sq, i, t, i == 0, False)
+
+        wa_grouped = [held([P, H, PACK], BF16, f"wa_grouped{a}") for a in range(PASSES)]
+        interleave(nc.vector.tensor_copy, wa_grouped[0][:], wa_raw[0][:])
+        wa_mx = [quantize(wa_grouped[0], H, "wa0")]
+        gather_scales(v_planes, v_tab_scales, idx, 0, S)
+        interleave(nc.scalar.copy, wa_grouped[1][:, 0:WA_SPLIT, :], wa_raw[1][:, :, 0:WA_SPLIT])
+        interleave(nc.vector.tensor_copy, wa_grouped[1][:, WA_SPLIT:H, :], wa_raw[1][:, :, WA_SPLIT:H])
+        wa_mx.append(quantize(wa_grouped[1], H, "wa1"))
+        for j0 in range(0, S, HALF):
+            gather_words(v_codes[0], v_tab[0], idx, j0, HALF)
+
+        mag = [[held([P, HALF], F32, f"mag{half}_{t}") for t in range(PACK)] for half in range(2)]
+        real_sq = [held([P, PACK, P], F32, f"real_sq{i}") for i in range(TILES)]
+
+        def real_tile(i):
+            acc = bank(i % 4, [P, H])
+            for a in range(PASSES):
+                real_pass(acc, i, a)
+            square(real_sq[i], acc)
+            if i < HALF_TILES:
+                for t in range(PACK):
+                    turn(totals[t], real_sq, i, t, False, i == HALF_TILES - 1)
+
+        def root(half, t, total):
+            nc.scalar.activation(mag[half][t][:], total[:], ACT.Sqrt)
+
+        for j0, n in SLICES:
+            gather_words(v_codes[1], v_tab[1], idx, j0, n)
+        for i in range(EARLY_TILES):
+            real_tile(i)
+        for t in range(PACK):
+            root(0, t, totals[t])
+            if EARLY_TILES + t < TILES:
+                real_tile(EARLY_TILES + t)
+        for t in range(PACK):
+            total = bank(4 + t, [P, HALF])
+            for part, sq in enumerate((imag_sq, real_sq)):
+                for i in range(HALF_TILES, TILES):
+                    turn(total, sq, i, t, part == 0 and i == HALF_TILES, part == 1 and i == TILES - 1)
+            root(1, t, total)
+
+        wm_grouped = held([P, N, PACK], BF16, "wm_grouped")
+        interleave(nc.vector.tensor_copy, wm_grouped[:], wm_raw[:])
+        wm_codes, wm_plane = quantize(wm_grouped, N, "wm")
+        out_rows = out.rearrange("(u p) j -> p u j", p=P)
+
+        def mask(h, h0, t, j0, n):
+            half, j = divmod(j0, HALF)
+            nc.vector.tensor_tensor(
+                h[:, t, j0 - h0 : j0 - h0 + n], picked(g_tab[t][:], idx, j0, n), mag[half][t][:, j : j + n], MULT
+            )
+
+        def mel_stage(c, h, h0):
+            j0, n = GROUPS[c]
+            j = j0 - h0
+            h_grouped = held([P, n, PACK], BF16, f"h_grouped{c}")
+            interleave(
+                nc.vector.tensor_copy if c in INTERLEAVE_ON_VECTOR else nc.scalar.copy, h_grouped[:], h[:, :, j : j + n]
+            )
+            h_codes, h_plane = quantize(h_grouped, n, f"h{c}")
+            mel = bank(c % 4, [P, N // P, n])
+            for u in range(N // P):
+                cols = slice(P * u, P * (u + 1))
+                nc.tensor.matmul_mx(
+                    out=mel[:, u, :],
+                    lhsT=wm_codes[:, cols].bitcast(FP8X4),
+                    lhsT_scale=wm_plane[:, cols],
+                    rhs=h_codes[:].bitcast(FP8X4),
+                    rhs_scale=h_plane[:],
+                    start=True,
+                    stop=True,
+                )
+            staged = held([P, N // P, n], F32, f"staged{c}")
+            copy_out = nc.vector.tensor_copy if c in COPY_OUT_ON_VECTOR else nc.scalar.copy
+            copy_out(out=staged[:], in_=mel[:])
+            nc.sync.dma_start(out_rows[:, :, j0 : j0 + n], staged[:])
+
+        for h0, width, slot in MASK_RUNS:
+            h = held([P, PACK, width], F32, f"h{h0}", tag=slot)
+            for t in range(PACK - 1):
+                mask(h, h0, t, h0, width)
+            for c, (j0, n) in enumerate(GROUPS):
+                if h0 <= j0 < h0 + width:
+                    mask(h, h0, PACK - 1, j0, n)
+                    mel_stage(c, h, h0)

@@ -23,13 +23,18 @@ PASSES = K // (P * PACK)
 TILES = S // P
 SLICES = [(0, 256), (256, 256), (512, 512)]
 V_ROW = 8
-MASK_RUNS = [(0, 512, None), (512, 256, "mag0_3"), (768, 256, "h_grouped1")]
+ORDER = "i2 i1 s2 s2 s2 s2 t2 wa sb sb sb t2 wb sh sb s1 s1 s1 s1 t1 wa t1 wm g g g g"
+INT = "VV"
+FIRST_SLICES = [(0, 512), (512, 512)]
+REAL_BANKS = (0, 1, 2, 3, 0, 3, 0, 3)
+SQUARE_ON_VECTOR = ()
+MASK_RUNS = [(0, 512, None), (512, 256, "mag0_3"), (768, 256, "h0")]
 EARLY_TILES = 5
 HALF = S // 2
 HALF_TILES = HALF // P
-WA_SPLIT = 128
+WA_SPLIT = 32
 GROUPS = [(0, 256), (256, 256), (512, 256), (768, 128), (896, 128)]
-INTERLEAVE_ON_VECTOR = (3, 4)
+INTERLEAVE_ON_VECTOR = (4,)
 COPY_OUT_ON_VECTOR = ()
 
 
@@ -87,11 +92,14 @@ def tile_list_masked_magnitude_mel_kernel(
         def table_words(words, a):
             return words[a].rearrange("p n t -> p (n t)").bitcast(I32)
 
-        def load_scales(queue, tile, scales, row):
-            for q in range(4):
-                queue.dma_start(
-                    tile[32 * q + row : 32 * q + row + 8, :], scales.bitcast(I32)[:, 4 * q : 4 * q + 4, :]
-                )
+        def load_scales(tile, scales, row, q):
+            nc.sync.dma_start(tile[32 * q + row : 32 * q + row + 8, :], scales.bitcast(I32)[:, 4 * q : 4 * q + 4, :])
+
+        def load_wb_scales(q):
+            nc.sync.dma_start(
+                wb_planes[32 * q : 32 * q + 4, :, :],
+                wb_scales.bitcast(I32)[:, 4 * q : 4 * q + 4, :].rearrange("a r c -> r a c"),
+            )
 
         def load_wa(a):
             nc.sync.dma_start(wa_raw[a][:], wa[512 * a : 512 * (a + 1), :].rearrange("(p j) r -> p j r", j=PACK))
@@ -110,29 +118,29 @@ def tile_list_masked_magnitude_mel_kernel(
             )
             return codes, plane
 
-        nc.sync.dma_start(idx2[:], offs2)
-        nc.sync.dma_start(idx[:], offs)
-        load_scales(nc.sync, v2_tab_scales, tab2_scales, 0)
-        nc.sync.dma_start(v2_tab[0][:], table_words(tab2_words, 0))
-        nc.sync.dma_start(wb_codes[:], wb_words.bitcast(I32).rearrange("a p c -> p a c"))
-        for q in range(4):
-            nc.sync.dma_start(
-                wb_planes[32 * q : 32 * q + 4, :, :],
-                wb_scales.bitcast(I32)[:, 4 * q : 4 * q + 4, :].rearrange("a r c -> r a c"),
-            )
-        nc.sync.dma_start(v2_tab[1][:], table_words(tab2_words, 1))
-        gather_scales(v2_planes, v2_tab_scales, idx2, 0, S)
-        nc.sync.dma_start(v2_plane1[0:112, :], v2_planes[4:116, :].bitcast(I32))
-        load_wa(0)
-        load_scales(nc.sync, v_tab_scales, tab_scales, V_ROW)
-        load_wa(1)
-        for a in range(PASSES):
-            nc.sync.dma_start(v_tab[a][:], table_words(tab_words, a))
+        def shift():
+            gather_scales(v2_planes, v2_tab_scales, idx2, 0, S)
+            nc.sync.dma_start(v2_plane1[0:112, :], v2_planes[4:116, :].bitcast(I32))
+
         g_planes = gT.rearrange("(p t) c -> t p c", t=PACK)
-        nc.sync.dma_start(g_tab[0][:], g_planes[0])
-        nc.sync.dma_start(wm_raw[:], wm.rearrange("(p j) n -> p j n", j=PACK))
-        for t in range(1, PACK):
-            nc.sync.dma_start(g_tab[t][:], g_planes[t])
+        loads = {
+            "i2": lambda n: nc.sync.dma_start(idx2[:], offs2),
+            "i1": lambda n: nc.sync.dma_start(idx[:], offs),
+            "s2": lambda n: load_scales(v2_tab_scales, tab2_scales, 0, n),
+            "s1": lambda n: load_scales(v_tab_scales, tab_scales, V_ROW, n),
+            "sb": load_wb_scales,
+            "t2": lambda n: nc.sync.dma_start(v2_tab[n][:], table_words(tab2_words, n)),
+            "t1": lambda n: nc.sync.dma_start(v_tab[n][:], table_words(tab_words, n)),
+            "wb": lambda n: nc.sync.dma_start(wb_codes[:], wb_words.bitcast(I32).rearrange("a p c -> p a c")),
+            "wa": load_wa,
+            "sh": lambda n: shift(),
+            "wm": lambda n: nc.sync.dma_start(wm_raw[:], wm.rearrange("(p j) n -> p j n", j=PACK)),
+            "g": lambda n: nc.sync.dma_start(g_tab[n][:], g_planes[n]),
+        }
+        seen = {}
+        for name in ORDER.split():
+            loads[name](seen.get(name, 0))
+            seen[name] = seen.get(name, 0) + 1
 
         def real_pass(acc, i, a):
             cols = slice(P * i, P * (i + 1))
@@ -159,8 +167,21 @@ def tile_list_masked_magnitude_mel_kernel(
                 stop=(a == PASSES - 1),
             )
 
-        def square(dst, acc):
-            nc.scalar.activation(dst[:], acc[:].rearrange("p (m t) -> p t m", t=PACK), ACT.Square)
+        def square_imag(dst, acc):
+            nc.scalar.activation(
+                dst[:].rearrange("p (u e) m -> p u m e", e=2),
+                acc[:].rearrange("p (m u e) -> p u m e", u=2, e=2),
+                ACT.Square,
+            )
+
+        def square_real(dst, acc, i):
+            flat = dst[:].rearrange("p t m -> p (t m)")
+            if i in SQUARE_ON_VECTOR:
+                plain = held([P, H], F32, f"real_sum{i}")
+                nc.vector.tensor_copy(plain[:], acc[:])
+                nc.vector.tensor_tensor(flat, plain[:], plain[:], MULT)
+            else:
+                nc.scalar.activation(flat, acc[:], ACT.Square)
 
         def turn(total, sq, i, t, first, last):
             j = P * (i % HALF_TILES)
@@ -178,7 +199,7 @@ def tile_list_masked_magnitude_mel_kernel(
             gather_words(v2_codes[1], v2_tab[1], idx2, j0, n)
             for i in range(j0 // P, (j0 + n) // P):
                 imag_pass(imag[i], i, 1)
-                square(imag_sq[i], imag[i])
+                square_imag(imag_sq[i], imag[i])
 
         totals = [bank(4 + t, [P, HALF]) for t in range(PACK)]
         for i in range(HALF_TILES):
@@ -186,23 +207,29 @@ def tile_list_masked_magnitude_mel_kernel(
                 turn(totals[t], imag_sq, i, t, i == 0, False)
 
         wa_grouped = [held([P, H, PACK], BF16, f"wa_grouped{a}") for a in range(PASSES)]
-        interleave(nc.vector.tensor_copy, wa_grouped[0][:], wa_raw[0][:])
+
+        def group_wa(copy, a, m0, m1):
+            copy(
+                out=wa_grouped[a][:].rearrange("p (t m) j -> p m j t", t=PACK)[:, m0:m1],
+                in_=wa_raw[a][:].rearrange("p j (m t) -> p m j t", t=PACK)[:, m0:m1],
+            )
+
+        group_wa(nc.scalar.copy if INT[0] == "S" else nc.vector.tensor_copy, 0, 0, P)
         wa_mx = [quantize(wa_grouped[0], H, "wa0")]
         gather_scales(v_planes, v_tab_scales, idx, 0, S)
-        interleave(nc.scalar.copy, wa_grouped[1][:, 0:WA_SPLIT, :], wa_raw[1][:, :, 0:WA_SPLIT])
-        interleave(nc.vector.tensor_copy, wa_grouped[1][:, WA_SPLIT:H, :], wa_raw[1][:, :, WA_SPLIT:H])
+        group_wa(nc.scalar.copy if INT[1] == "S" else nc.vector.tensor_copy, 1, 0, P)
         wa_mx.append(quantize(wa_grouped[1], H, "wa1"))
-        for j0 in range(0, S, HALF):
-            gather_words(v_codes[0], v_tab[0], idx, j0, HALF)
+        for j0, n in FIRST_SLICES:
+            gather_words(v_codes[0], v_tab[0], idx, j0, n)
 
         mag = [[held([P, HALF], F32, f"mag{half}_{t}") for t in range(PACK)] for half in range(2)]
         real_sq = [held([P, PACK, P], F32, f"real_sq{i}") for i in range(TILES)]
 
         def real_tile(i):
-            acc = bank(i % 4, [P, H])
+            acc = bank(REAL_BANKS[i], [P, H])
             for a in range(PASSES):
                 real_pass(acc, i, a)
-            square(real_sq[i], acc)
+            square_real(real_sq[i], acc, i)
             if i < HALF_TILES:
                 for t in range(PACK):
                     turn(totals[t], real_sq, i, t, False, i == HALF_TILES - 1)
@@ -244,7 +271,7 @@ def tile_list_masked_magnitude_mel_kernel(
                 nc.vector.tensor_copy if c in INTERLEAVE_ON_VECTOR else nc.scalar.copy, h_grouped[:], h[:, :, j : j + n]
             )
             h_codes, h_plane = quantize(h_grouped, n, f"h{c}")
-            mel = bank(c % 4, [P, N // P, n])
+            mel = bank(1 + c % 2, [P, N // P, n])
             for u in range(N // P):
                 cols = slice(P * u, P * (u + 1))
                 nc.tensor.matmul_mx(

from contextlib import ExitStack

import concourse.mybir as mybir
from concourse.masks import make_identity

K, T, S, H, N = 1024, 2048, 1024, 512, 256
FLOPS = 2 * (2 * K * H * S + H * N * S)

F32 = mybir.dt.float32
BF16 = mybir.dt.bfloat16
I32 = mybir.dt.int32
U32 = mybir.dt.uint32
U16 = mybir.dt.uint16
U8 = mybir.dt.uint8
FP8X4 = mybir.dt.float8_e4m3fn_x4
FP4X4 = mybir.dt.float4_e2m1fn_x4
ACT = mybir.ActivationFunctionType
MULT = mybir.AluOpType.mult

P = 128
PACK = 4
PASSES = K // (P * PACK)
TILES = S // P
SLICES = [(0, 256), (256, 256), (512, 512)]
V_ROW = 8
ORDER = "i2 i1 s2 s2 s2 s2 t2 wa sb sb sb t2 wb sh sb s1 s1 s1 s1 t1 wa t1 wm g g g g"
INT = "VV"
FIRST_SLICES = [(0, 512), (512, 512)]
REAL_BANKS = (0, 1, 2, 3, 0, 3, 0, 3)
SQUARE_ON_VECTOR = ()
MASK_RUNS = [(0, 512, None), (512, 256, "mag0_3"), (768, 256, "h0")]
EARLY_TILES = 5
HALF = S // 2
HALF_TILES = HALF // P
WA_SPLIT = 32
GROUPS = [(0, 256), (256, 256), (512, 256), (768, 128), (896, 128)]
INTERLEAVE_ON_VECTOR = (4,)
COPY_OUT_ON_VECTOR = ()


def picked(window, offsets, j0, n):
    return window.indirect(offsets[:, j0 // 16 : (j0 + n) // 16])


def interleave(copy, grouped, planes):
    copy(
        out=grouped.rearrange("p (c i) t -> p c t i", i=4),
        in_=planes.rearrange("p t (c i) -> p c t i", i=4),
    )


def tile_list_masked_magnitude_mel_kernel(
    tc, tab_words, tab_scales, tab2_words, tab2_scales, offs, offs2, wa, wb_words, wb_scales, gT, wm, out
):
    nc = tc.nc
    with ExitStack() as ctx:
        keep = ctx.enter_context(tc.tile_pool(name="keep", bufs=1))
        psum = ctx.enter_context(tc.psum_pool(name="psum", bufs=1))

        def held(shape, dtype, name, tag=None):
            return keep.tile(shape, dtype, name=name, tag=tag or name, align_bytes=64)

        def bank(b, shape):
            return psum.tile(shape, F32, name=f"bank{b}")

        idx = keep.tile([P, S // 16], U16, name="idx")
        idx2 = keep.tile([P, S // 16], U16, name="idx2")
        v_tab = [held([P, T], I32, f"v_tab{a}") for a in range(PASSES)]
        v2_tab = [held([P, T], I32, f"v2_tab{a}") for a in range(PASSES)]
        g_tab = [held([P, T], F32, f"g_tab{t}") for t in range(PACK)]
        wa_raw = [held([P, PACK, H], F32, f"wa_raw{a}") for a in range(PASSES)]
        wm_raw = held([P, PACK, N], F32, "wm_raw")
        wb_codes = held([P, PASSES, H // 2], I32, "wb_codes")
        v_tab_scales = held([P, T // 4], I32, "v_tab_scales")
        v2_tab_scales = held([P, T // 4], I32, "v2_tab_scales")
        wb_planes = held([P, PASSES, H // 4], I32, "wb_planes")
        v2_plane1 = held([P, S // 4], I32, "v2_plane1")
        v_codes = [held([P, S], U32, f"v_codes{a}") for a in range(PASSES)]
        v2_codes = [held([P, S], U32, f"v2_codes{a}") for a in range(PASSES)]
        v_planes = held([P, S], U8, "v_planes")
        v2_planes = held([P, S], U8, "v2_planes")

        nc.gpsimd.memset(v2_tab_scales[:], 0)
        nc.vector.memset(wb_planes[:], 0)
        nc.vector.memset(v_tab_scales[:], 0)
        nc.vector.memset(v2_plane1[96:P, :], 0)
        ident = held([P, P], F32, "ident")
        make_identity(nc, ident[:])
        warm = held([P, 1], F32, "warm")
        nc.scalar.activation(warm[:], ident[:, 0:1], ACT.Sqrt)

        def table_words(words, a):
            return words[a].rearrange("p n t -> p (n t)").bitcast(I32)

        def load_scales(tile, scales, row, q):
            nc.sync.dma_start(tile[32 * q + row : 32 * q + row + 8, :], scales.bitcast(I32)[:, 4 * q : 4 * q + 4, :])

        def load_wb_scales(q):
            nc.sync.dma_start(
                wb_planes[32 * q : 32 * q + 4, :, :],
                wb_scales.bitcast(I32)[:, 4 * q : 4 * q + 4, :].rearrange("a r c -> r a c"),
            )

        def load_wa(a):
            nc.sync.dma_start(wa_raw[a][:], wa[512 * a : 512 * (a + 1), :].rearrange("(p j) r -> p j r", j=PACK))

        def gather_words(dst, table, offsets, j0, n):
            nc.vector.tensor_copy(dst[:, j0 : j0 + n], picked(table[:].bitcast(U32), offsets, j0, n))

        def gather_scales(dst, table, offsets, j0, n):
            nc.vector.tensor_copy(dst[:, j0 : j0 + n], picked(table[:].bitcast(U8), offsets, j0, n))

        def quantize(grouped, width, name):
            codes = held([P, width], U32, name + "_codes")
            plane = held([P, width], U8, name + "_plane")
            nc.vector.quantize_mx(
                out=codes[:].bitcast(FP8X4), scales=plane[:], in_=grouped[:].rearrange("p w t -> p (w t)")
            )
            return codes, plane

        def shift():
            gather_scales(v2_planes, v2_tab_scales, idx2, 0, S)
            nc.sync.dma_start(v2_plane1[0:112, :], v2_planes[4:116, :].bitcast(I32))

        g_planes = gT.rearrange("(p t) c -> t p c", t=PACK)
        loads = {
            "i2": lambda n: nc.sync.dma_start(idx2[:], offs2),
            "i1": lambda n: nc.sync.dma_start(idx[:], offs),
            "s2": lambda n: load_scales(v2_tab_scales, tab2_scales, 0, n),
            "s1": lambda n: load_scales(v_tab_scales, tab_scales, V_ROW, n),
            "sb": load_wb_scales,
            "t2": lambda n: nc.sync.dma_start(v2_tab[n][:], table_words(tab2_words, n)),
            "t1": lambda n: nc.sync.dma_start(v_tab[n][:], table_words(tab_words, n)),
            "wb": lambda n: nc.sync.dma_start(wb_codes[:], wb_words.bitcast(I32).rearrange("a p c -> p a c")),
            "wa": load_wa,
            "sh": lambda n: shift(),
            "wm": lambda n: nc.sync.dma_start(wm_raw[:], wm.rearrange("(p j) n -> p j n", j=PACK)),
            "g": lambda n: nc.sync.dma_start(g_tab[n][:], g_planes[n]),
        }
        seen = {}
        for name in ORDER.split():
            loads[name](seen.get(name, 0))
            seen[name] = seen.get(name, 0) + 1

        def real_pass(acc, i, a):
            cols = slice(P * i, P * (i + 1))
            nc.tensor.matmul_mx(
                out=acc[:],
                lhsT=v_codes[a][:, cols].bitcast(FP8X4),
                lhsT_scale=v_planes[V_ROW + 4 * a : P, cols],
                rhs=wa_mx[a][0][:].bitcast(FP8X4),
                rhs_scale=wa_mx[a][1][:],
                start=(a == 0),
                stop=(a == PASSES - 1),
            )

        def imag_pass(acc, i, a):
            cols = slice(P * i, P * (i + 1))
            plane = v2_planes[:] if a == 0 else v2_plane1[:].bitcast(U8)
            nc.tensor.matmul_mx(
                out=acc[:],
                lhsT=v2_codes[a][:, cols].bitcast(FP8X4),
                lhsT_scale=plane[:, cols],
                rhs=wb_codes[:, a, :].bitcast(FP4X4),
                rhs_scale=wb_planes[:, a, :].bitcast(U8),
                start=(a == 0),
                stop=(a == PASSES - 1),
            )

        def square_imag(dst, acc):
            nc.scalar.activation(
                dst[:].rearrange("p (u e) m -> p u m e", e=2),
                acc[:].rearrange("p (m u e) -> p u m e", u=2, e=2),
                ACT.Square,
            )

        def square_real(dst, acc, i):
            flat = dst[:].rearrange("p t m -> p (t m)")
            if i in SQUARE_ON_VECTOR:
                plain = held([P, H], F32, f"real_sum{i}")
                nc.vector.tensor_copy(plain[:], acc[:])
                nc.vector.tensor_tensor(flat, plain[:], plain[:], MULT)
            else:
                nc.scalar.activation(flat, acc[:], ACT.Square)

        def turn(total, sq, i, t, first, last):
            j = P * (i % HALF_TILES)
            nc.tensor.matmul(
                total[:, j : j + P], lhsT=sq[i][:, t, :], rhs=ident[:], is_transpose=True, start=first, stop=last
            )

        imag = [bank((i + 4) % 8, [P, H]) for i in range(TILES)]
        for j0 in range(0, S, HALF):
            gather_words(v2_codes[0], v2_tab[0], idx2, j0, HALF)
            for i in range(j0 // P, (j0 + HALF) // P):
                imag_pass(imag[i], i, 0)
        imag_sq = [held([P, PACK, P], F32, f"imag_sq{i}") for i in range(TILES)]
        for j0, n in SLICES:
            gather_words(v2_codes[1], v2_tab[1], idx2, j0, n)
            for i in range(j0 // P, (j0 + n) // P):
                imag_pass(imag[i], i, 1)
                square_imag(imag_sq[i], imag[i])

        totals = [bank(4 + t, [P, HALF]) for t in range(PACK)]
        for i in range(HALF_TILES):
            for t in range(PACK):
                turn(totals[t], imag_sq, i, t, i == 0, False)

        wa_grouped = [held([P, H, PACK], BF16, f"wa_grouped{a}") for a in range(PASSES)]

        def group_wa(copy, a, m0, m1):
            copy(
                out=wa_grouped[a][:].rearrange("p (t m) j -> p m j t", t=PACK)[:, m0:m1],
                in_=wa_raw[a][:].rearrange("p j (m t) -> p m j t", t=PACK)[:, m0:m1],
            )

        group_wa(nc.scalar.copy if INT[0] == "S" else nc.vector.tensor_copy, 0, 0, P)
        wa_mx = [quantize(wa_grouped[0], H, "wa0")]
        gather_scales(v_planes, v_tab_scales, idx, 0, S)
        group_wa(nc.scalar.copy if INT[1] == "S" else nc.vector.tensor_copy, 1, 0, P)
        wa_mx.append(quantize(wa_grouped[1], H, "wa1"))
        for j0, n in FIRST_SLICES:
            gather_words(v_codes[0], v_tab[0], idx, j0, n)

        mag = [[held([P, HALF], F32, f"mag{half}_{t}") for t in range(PACK)] for half in range(2)]
        real_sq = [held([P, PACK, P], F32, f"real_sq{i}") for i in range(TILES)]

        def real_tile(i):
            acc = bank(REAL_BANKS[i], [P, H])
            for a in range(PASSES):
                real_pass(acc, i, a)
            square_real(real_sq[i], acc, i)
            if i < HALF_TILES:
                for t in range(PACK):
                    turn(totals[t], real_sq, i, t, False, i == HALF_TILES - 1)

        def root(half, t, total):
            nc.scalar.activation(mag[half][t][:], total[:], ACT.Sqrt)

        for j0, n in SLICES:
            gather_words(v_codes[1], v_tab[1], idx, j0, n)
        for i in range(EARLY_TILES):
            real_tile(i)
        for t in range(PACK):
            root(0, t, totals[t])
            if EARLY_TILES + t < TILES:
                real_tile(EARLY_TILES + t)
        for t in range(PACK):
            total = bank(4 + t, [P, HALF])
            for part, sq in enumerate((imag_sq, real_sq)):
                for i in range(HALF_TILES, TILES):
                    turn(total, sq, i, t, part == 0 and i == HALF_TILES, part == 1 and i == TILES - 1)
            root(1, t, total)

        wm_grouped = held([P, N, PACK], BF16, "wm_grouped")
        interleave(nc.vector.tensor_copy, wm_grouped[:], wm_raw[:])
        wm_codes, wm_plane = quantize(wm_grouped, N, "wm")
        out_rows = out.rearrange("(u p) j -> p u j", p=P)

        def mask(h, h0, t, j0, n):
            half, j = divmod(j0, HALF)
            nc.vector.tensor_tensor(
                h[:, t, j0 - h0 : j0 - h0 + n], picked(g_tab[t][:], idx, j0, n), mag[half][t][:, j : j + n], MULT
            )

        def mel_stage(c, h, h0):
            j0, n = GROUPS[c]
            j = j0 - h0
            h_grouped = held([P, n, PACK], BF16, f"h_grouped{c}")
            interleave(
                nc.vector.tensor_copy if c in INTERLEAVE_ON_VECTOR else nc.scalar.copy, h_grouped[:], h[:, :, j : j + n]
            )
            h_codes, h_plane = quantize(h_grouped, n, f"h{c}")
            mel = bank(1 + c % 2, [P, N // P, n])
            for u in range(N // P):
                cols = slice(P * u, P * (u + 1))
                nc.tensor.matmul_mx(
                    out=mel[:, u, :],
                    lhsT=wm_codes[:, cols].bitcast(FP8X4),
                    lhsT_scale=wm_plane[:, cols],
                    rhs=h_codes[:].bitcast(FP8X4),
                    rhs_scale=h_plane[:],
                    start=True,
                    stop=True,
                )
            staged = held([P, N // P, n], F32, f"staged{c}")
            copy_out = nc.vector.tensor_copy if c in COPY_OUT_ON_VECTOR else nc.scalar.copy
            copy_out(out=staged[:], in_=mel[:])
            nc.sync.dma_start(out_rows[:, :, j0 : j0 + n], staged[:])

        for h0, width, slot in MASK_RUNS:
            h = held([P, PACK, width], F32, f"h{h0}", tag=slot)
            for t in range(PACK - 1):
                mask(h, h0, t, h0, width)
            for c, (j0, n) in enumerate(GROUPS):
                if h0 <= j0 < h0 + width:
                    mask(h, h0, PACK - 1, j0, n)
                    mel_stage(c, h, h0)
